import numpy as np
CORES = [4,20,60,84,92,100,116]
N = 7
TK = 64
def setup_inputs(rng):
    return {"b": rng.standard_normal((N, 128, TK), dtype=np.float32), "l": (rng.standard_normal((N, 128, N * 128), dtype=np.float32) / 16)}
def setup_inputs_big(rng):
    d = setup_inputs(rng)
    for k in ("b",): d[k] = (d[k].astype(np.float32) * 1048576.0).astype(d[k].dtype)
    return d
def setup_inputs_small(rng):
    d = setup_inputs(rng)
    for k in ("b",): d[k] = (d[k].astype(np.float32) * (1 / 1048576.0)).astype(d[k].dtype)
    return d
def setup_inputs_apart(rng):
    d = setup_inputs(rng)
    f = (10.0 ** rng.permutation(np.linspace(-1.5, 1.5, N))).astype(np.float32).reshape(N, 1, 1)
    for k in ("b",): d[k] = (d[k].astype(np.float32) * f).astype(d[k].dtype)
    return d
def reference(b, l):
    B, L = b.astype(np.float64), l.astype(np.float64)
    y = np.zeros((N, 128, TK))
    for r in range(N):
        acc = B[r].copy()
        for s in range(r):
            acc -= L[r][:, 128 * s:128 * s + 128].T @ y[s]
        y[r] = acc
    return {"y": y.astype(np.float32)}

@@ -1,0 +1,232 @@
+from concourse.bass import DstId, RemoteDMATransfer
+from concourse.mybir import AluOpType
+
+P = 128
+K = 64
+NT = 6
+
+
+def _col(s):
+    return K + P * s
+
+
+SCRATCH = {
+    "own": ("sbuf", [P, K + NT * P], "float32"),
+    "row2": ("sbuf", [P, K + 2 * P], "float32"),
+    "y01": ("sbuf", [P, 2 * K], "float32"),
+    "c24": ("sbuf", [P, 2 * K], "float32"),
+    "c3": ("sbuf", [P, K], "float32"),
+    "c5": ("sbuf", [P, K], "float32"),
+    "c6": ("sbuf", [P, K], "float32"),
+    "a32": ("sbuf", [P, P], "float32"),
+    "a4x": ("sbuf", [P, 2 * P], "float32"),
+    "a5x": ("sbuf", [P, 3 * P], "float32"),
+    "yy": ("sbuf", [P, 4 * K], "float32"),
+    "psc": ("psum", [P, 512], "float32"),
+    "ps3": ("psum", [P, 512], "float32"),
+    "ps4": ("psum", [P, 512], "float32"),
+    "ps5": ("psum", [P, 512], "float32"),
+    "ps6": ("psum", [P, 512], "float32"),
+}
+SEMAPHORES = ["ldA", "ldB", "st", "sent",
+              "s_b0", "s_row", "s_rowA", "s_row2", "s_y01", "s_a32", "s_a4x", "s_a5x", "s_c3", "s_c5", "s_c24",
+              "mmc", "cv", "mm3", "mm4", "mm5", "mm6", "yv3", "yv4", "yv5", "yv6"]
+
+NE = 8
+
+
+def _low_bits(mask, n):
+    out, got, bit = 0, 0, 1
+    while got < n:
+        if mask & bit:
+            out |= bit
+            got += 1
+        bit <<= 1
+    return out
+
+
+def _helpers(c, T, topo):
+    far = [x for x in T.cores
+           if topo.chip(x) != topo.chip(c) and not topo.same_plane(topo.chip(x), topo.chip(c))]
+    return [h for h in range(topo.CHIPS * topo.CORES_PER_CHIP)
+            if topo.chip(h) == topo.chip(c) and topo.die(h) == topo.die(c) and h not in T.cores
+            and all(topo.may_write(h, x) for x in far)]
+
+
+def rank_program(g, core, T, topo):
+    R = list(T.cores)
+    H1 = _helpers(R[1], T, topo)[0]
+    H3 = _helpers(R[3], T, topo)[0]
+    H4a, H4b = _helpers(R[4], T, topo)[0:2]
+    if core not in R and core not in (H1, H3, H4a, H4b):
+        return
+    S = T.sem
+    sent = [0]
+
+    def send(src, dst, dsts, sem):
+        mask = topo.mask(core, dsts[0])
+        for d in dsts:
+            mask &= topo.mask(core, d)
+        mask = _low_bits(mask, NE)
+        if len(dsts) == 1:
+            rid, pid, _se = topo.addr(dsts[0])
+            g.remote_dma(out_ap=dst, in_ap=src, remote_sem=sem, local_sem=S.sent, pid=pid, routing_id=rid,
+                         dma_engine_mask=mask)
+        else:
+            ids = [DstId(rid=topo.addr(d)[0], pnc=topo.addr(d)[1]) for d in dsts]
+            g.remote_dma_fused([RemoteDMATransfer(dst_ids=ids, dma_engine_mask=mask, remote_sem=sem, srcs=[src],
+                                                  dsts=[dst for _d in dsts], alu_op=0)], local_sem=S.sent)
+        sent[0] += NE
+
+    def finish(stored):
+        if sent[0]:
+            g.wait_ge(S.sent, sent[0])
+        if stored:
+            g.wait_ge(S.st, 16)
+
+    def store(src, sem):
+        g.sync.wait_ge(sem, 1)
+        g.sync.dma_start(T.y[:, :], src).then_inc(S.st, 16)
+
+    def load_b_part(ntiles):
+        g.sync.dma_start(T.own[:, 0:K], T.b[:, :]).then_inc(S.ldB, 16)
+        g.scalar.dma_start(T.own[:, K:_col(ntiles)], T.l[:, 0:P * ntiles]).then_inc(S.ldB, 16)
+
+    def load_a_part(r):
+        g.sync.dma_start(T.own[:, _col(2):_col(r)], T.l[:, P * 2:P * r]).then_inc(S.ldA, 16)
+
+    def partial(row, row_sem, row_val, ps, out, mm_sem, ntiles=2):
+        g.tensor.wait_ge(row_sem, row_val)
+        for s in range(ntiles):
+            mm = g.tensor.matmul(ps[:, 0:K], row[:, _col(s):_col(s + 1)], T.y01[:, K * s:K * (s + 1)],
+                                 s == 0, s == ntiles - 1)
+        mm.then_inc(mm_sem, 1)
+        g.vector.wait_ge(row_sem, row_val)
+        g.vector.wait_ge(mm_sem, 1)
+        g.vector.tensor_tensor(out, row[:, 0:K], ps[:, 0:K], AluOpType.subtract).then_inc(S.cv, 1)
+
+    def solve_group(r):
+        ps = {3: T.ps3, 4: T.ps4, 5: T.ps5, 6: T.ps6}
+        mms = {3: S.mm3, 4: S.mm4, 5: S.mm5, 6: S.mm6}
+        yvs = {3: S.yv3, 4: S.yv4, 5: S.yv5, 6: S.yv6}
+        land = {3: (T.a32, S.s_a32), 4: (T.a4x, S.s_a4x), 5: (T.a5x, S.s_a5x)}
+        cs = {3: (T.c3[:, :], S.s_c3, NE), 4: (T.c24[:, K:2 * K], S.s_c24, NE), 5: (T.c5[:, :], S.s_c5, NE)}
+        if r == 5:
+            cs[5] = (T.c5[:, :], S.cv, 1)
+        if r == 6:
+            cs[6] = (T.c6[:, :], S.cv, 1)
+
+        def y(s):
+            return T.c24[:, 0:K] if s == 2 else T.yy[:, K * (s - 3):K * (s - 2)]
+
+        g.tensor.wait_ge(S.s_c24, NE)
+        for q in range(3, r + 1):
+            if q == r:
+                g.tensor.wait_ge(S.ldA, 16)
+            else:
+                g.tensor.wait_ge(land[q][1], NE)
+            for s in range(2, q):
+                if q == r:
+                    tile = T.own[:, _col(s):_col(s + 1)]
+                else:
+                    tile = land[q][0][:, P * (s - 2):P * (s - 1)]
+                if s == q - 1 and s >= 3:
+                    g.tensor.wait_ge(yvs[s], 1)
+                mm = g.tensor.matmul(ps[q][:, 0:K], tile, y(s), s == 2, s == q - 1)
+            mm.then_inc(mms[q], 1)
+            c_ap, c_sem, c_val = cs[q]
+            g.vector.wait_ge(c_sem, c_val)
+            g.vector.wait_ge(mms[q], 1)
+            g.vector.tensor_tensor(y(q), c_ap, ps[q][:, 0:K], AluOpType.subtract).then_inc(yvs[q], 1)
+        store(y(r), yvs[r])
+
+    if core == R[0]:
+        g.sync.dma_start(T.own[:, 0:K], T.b[:, :]).then_inc(S.ldB, 16)
+        g.scalar.dma_start(T.y[:, :], T.b[:, :]).then_inc(S.st, 16)
+        g.wait_ge(S.ldB, 16)
+        send(T.own[:, 0:K], T.y01[:, 0:K], [H1, R[1]], S.s_b0)
+        finish(True)
+
+    elif core in (R[1], H1):
+        mine = core == R[1]
+        if mine:
+            load_b_part(1)
+            g.wait_ge(S.ldB, 32)
+            send(T.own[:, 0:_col(1)], T.own[:, 0:_col(1)], [H1], S.s_row)
+        g.tensor.wait_ge(S.s_b0, NE)
+        partial(T.own, S.ldB if mine else S.s_row, 32 if mine else NE, T.psc, T.y01[:, K:2 * K], S.mmc, ntiles=1)
+        if mine:
+            store(T.y01[:, K:2 * K], S.cv)
+        g.wait_ge(S.s_b0, NE)
+        g.wait_ge(S.cv, 1)
+        send(T.y01[:, :], T.y01[:, :], [H3, R[5], R[6]] if mine else [H4a, H4b, R[2]], S.s_y01)
+        finish(mine)
+
+    elif core == R[2]:
+        load_b_part(2)
+        g.wait_ge(S.ldB, 32)
+        send(T.own[:, 0:_col(2)], T.row2[:, :], [H4a, H4b], S.s_row2)
+        g.tensor.wait_ge(S.s_y01, NE)
+        partial(T.own, S.ldB, 32, T.psc, T.yy[:, 0:K], S.mmc)
+        store(T.yy[:, 0:K], S.cv)
+        finish(True)
+
+    elif core == R[3]:
+        load_b_part(2)
+        load_a_part(3)
+        g.wait_ge(S.ldB, 32)
+        g.wait_ge(S.ldA, 16)
+        send(T.own[:, 0:_col(3)], T.own[:, 0:_col(3)], [H3], S.s_row)
+        send(T.own[:, _col(2):_col(3)], T.a32[:, :], [R[6], R[5]], S.s_a32)
+        solve_group(3)
+        finish(True)
+
+    elif core == H3:
+        g.wait_ge(S.s_row, NE)
+        send(T.own[:, _col(2):_col(3)], T.a32[:, :], [R[4]], S.s_a32)
+        g.tensor.wait_ge(S.s_y01, NE)
+        partial(T.own, S.s_row, NE, T.psc, T.c3[:, :], S.mmc)
+        g.wait_ge(S.cv, 1)
+        send(T.c3[:, :], T.c3[:, :], [R[4], R[6], R[5], R[3]], S.s_c3)
+        finish(False)
+
+    elif core == R[4]:
+        load_a_part(4)
+        load_b_part(2)
+        g.wait_ge(S.ldA, 16)
+        send(T.own[:, _col(2):_col(4)], T.own[:, _col(2):_col(4)], [H4a, H4b], S.s_rowA)
+        g.wait_ge(S.ldB, 32)
+        send(T.own[:, 0:_col(2)], T.own[:, 0:_col(2)], [H4a, H4b], S.s_row)
+        solve_group(4)
+        finish(True)
+
+    elif core in (H4a, H4b):
+        first = core == H4a
+        g.wait_ge(S.s_rowA, NE)
+        send(T.own[:, _col(2):_col(4)], T.a4x[:, :], [R[6] if first else R[5]], S.s_a4x)
+        g.tensor.wait_ge(S.s_y01, NE)
+        partial(T.row2, S.s_row2, NE, T.psc, T.c24[:, 0:K], S.mmc)
+        partial(T.own, S.s_row, NE, T.ps4, T.c24[:, K:2 * K], S.mm4)
+        g.wait_ge(S.cv, 2)
+        send(T.c24[:, :], T.c24[:, :], [R[6], R[4]] if first else [R[5], R[3]], S.s_c24)
+        finish(False)
+
+    elif core == R[5]:
+        load_a_part(5)
+        load_b_part(2)
+        g.wait_ge(S.ldA, 16)
+        send(T.own[:, _col(2):_col(5)], T.a5x[:, :], [R[6]], S.s_a5x)
+        g.tensor.wait_ge(S.s_y01, NE)
+        partial(T.own, S.ldB, 32, T.psc, T.c5[:, :], S.mmc)
+        g.wait_ge(S.cv, 1)
+        send(T.c5[:, :], T.c5[:, :], [R[6]], S.s_c5)
+        solve_group(5)
+        finish(True)
+
+    elif core == R[6]:
+        load_b_part(2)
+        load_a_part(6)
+        g.tensor.wait_ge(S.s_y01, NE)
+        partial(T.own, S.ldB, 32, T.psc, T.c6[:, :], S.mmc)
+        solve_group(6)
+        finish(True)

@@ -4,6 +4,7 @@ from concourse.mybir import AluOpType
 P = 128
 K = 64
 NT = 6
+FOLD42 = True
 
 
 def _col(s):
@@ -22,15 +23,23 @@ SCRATCH = {
     "a4x": ("sbuf", [P, 2 * P], "float32"),
     "a5x": ("sbuf", [P, 3 * P], "float32"),
     "yy": ("sbuf", [P, 4 * K], "float32"),
+    "eye_src": ("sbuf", [P, P + 1], "float32"),
+    "eye_d": ("dram", [P + 1, P], "float32"),
+    "eye": ("sbuf", [P, P], "float32"),
+    "t5": ("sbuf", [P, 3 * P], "float32"),
+    "u6": ("sbuf", [P, 3 * P], "float32"),
     "psc": ("psum", [P, 512], "float32"),
     "ps3": ("psum", [P, 512], "float32"),
     "ps4": ("psum", [P, 512], "float32"),
     "ps5": ("psum", [P, 512], "float32"),
     "ps6": ("psum", [P, 512], "float32"),
+    "pt": ("psum", [P, 512], "float32"),
+    "pu": ("psum", [P, 512], "float32"),
 }
 SEMAPHORES = ["ldA", "ldB", "st", "sent",
-              "s_b0", "s_row", "s_rowA", "s_row2", "s_y01", "s_a32", "s_a4x", "s_a5x", "s_c3", "s_c5", "s_c24",
-              "mmc", "cv", "mm3", "mm4", "mm5", "mm6", "yv3", "yv4", "yv5", "yv6"]
+              "s_b0", "s_row1", "s_row", "s_rowA", "s_row2", "s_y01", "s_a32", "s_a4x", "s_a5x", "s_c3", "s_c5", "s_c2",
+              "s_c4", "mmc", "cv", "cv2", "mm3", "mm4", "mm5", "mm6", "yv3", "yv4", "yv5", "yv6",
+              "ms", "ed", "ed2", "tp", "tc", "up", "uc"]
 
 NE = 8
 
@@ -62,21 +71,38 @@ def rank_program(g, core, T, topo):
         return
     S = T.sem
     sent = [0]
+    SUB = AluOpType.subtract
 
-    def send(src, dst, dsts, sem):
+    def common_mask(dsts):
         mask = topo.mask(core, dsts[0])
         for d in dsts:
             mask &= topo.mask(core, d)
-        mask = _low_bits(mask, NE)
+        return mask
+
+    def dst_id(d):
+        return DstId(rid=topo.addr(d)[0], pnc=topo.addr(d)[1])
+
+    def send(src, dst, dsts, sem):
+        mask = _low_bits(common_mask(dsts), NE)
         if len(dsts) == 1:
             rid, pid, _se = topo.addr(dsts[0])
             g.remote_dma(out_ap=dst, in_ap=src, remote_sem=sem, local_sem=S.sent, pid=pid, routing_id=rid,
                          dma_engine_mask=mask)
         else:
-            ids = [DstId(rid=topo.addr(d)[0], pnc=topo.addr(d)[1]) for d in dsts]
-            g.remote_dma_fused([RemoteDMATransfer(dst_ids=ids, dma_engine_mask=mask, remote_sem=sem, srcs=[src],
-                                                  dsts=[dst for _d in dsts], alu_op=0)], local_sem=S.sent)
+            g.remote_dma_fused([RemoteDMATransfer(dst_ids=[dst_id(d) for d in dsts], dma_engine_mask=mask, remote_sem=sem,
+                                                  srcs=[src], dsts=[dst for _d in dsts], alu_op=0)], local_sem=S.sent)
         sent[0] += NE
+
+    def send_each(src, dst, dsts, sem):
+        mask = common_mask(dsts)
+        trs = []
+        for d in dsts:
+            part = _low_bits(mask, NE)
+            mask &= ~part
+            trs.append(RemoteDMATransfer(dst_ids=[dst_id(d)], dma_engine_mask=part, remote_sem=sem, srcs=[src],
+                                         dsts=[dst], alu_op=0))
+            sent[0] += NE
+        g.remote_dma_fused(trs, local_sem=S.sent)
 
     def finish(stored):
         if sent[0]:
@@ -103,41 +129,63 @@ def rank_program(g, core, T, topo):
         mm.then_inc(mm_sem, 1)
         g.vector.wait_ge(row_sem, row_val)
         g.vector.wait_ge(mm_sem, 1)
-        g.vector.tensor_tensor(out, row[:, 0:K], ps[:, 0:K], AluOpType.subtract).then_inc(S.cv, 1)
+        g.vector.tensor_tensor(out, row[:, 0:K], ps[:, 0:K], SUB).then_inc(S.cv, 1)
 
     def solve_group(r):
         ps = {3: T.ps3, 4: T.ps4, 5: T.ps5, 6: T.ps6}
         mms = {3: S.mm3, 4: S.mm4, 5: S.mm5, 6: S.mm6}
         yvs = {3: S.yv3, 4: S.yv4, 5: S.yv5, 6: S.yv6}
-        land = {3: (T.a32, S.s_a32), 4: (T.a4x, S.s_a4x), 5: (T.a5x, S.s_a5x)}
-        cs = {3: (T.c3[:, :], S.s_c3, NE), 4: (T.c24[:, K:2 * K], S.s_c24, NE), 5: (T.c5[:, :], S.s_c5, NE)}
-        if r == 5:
-            cs[5] = (T.c5[:, :], S.cv, 1)
-        if r == 6:
-            cs[6] = (T.c6[:, :], S.cv, 1)
+        cs = {3: (T.c3[:, :], S.s_c3, NE), 4: (T.c24[:, K:2 * K], S.s_c4, NE), 5: (T.c5[:, :], S.cv, 1),
+              6: (T.c6[:, :], S.cv, 1)}
 
         def y(s):
             return T.c24[:, 0:K] if s == 2 else T.yy[:, K * (s - 3):K * (s - 2)]
 
-        g.tensor.wait_ge(S.s_c24, NE)
-        for q in range(3, r + 1):
+        def operand(q, s):
+            if q == 6 and s < 5:
+                return T.u6[:, P * (s - 2):P * (s - 1)], "uc", 1
             if q == r:
-                g.tensor.wait_ge(S.ldA, 16)
+                return T.own[:, _col(s):_col(s + 1)], "ldA", 16
+            if q == 3:
+                return T.a32[:, :], "s_a32", NE
+            return T.a4x[:, P * (s - 2):P * (s - 1)], "s_a4x", NE
+
+        if FOLD42:
+            seq = [(3, 2), (r, 2), (4, 3), (r, 3), (r, 5), (r, 4)]
+        else:
+            seq = [(3, 2), (4, 2), (4, 3), (r, 2), (r, 3), (r, 5), (r, 4)]
+        seq = [(q, s) for i, (q, s) in enumerate(seq) if q <= r and s < q and (q, s) not in seq[:i]
+               and not (FOLD42 and (q, s) == (4, 2))]
+        rows = [q for q in (3, 4, 5, 6) if q <= min(r, 4) or q == r]
+        seen = []
+
+        def twait(name, val):
+            if name not in seen:
+                seen.append(name)
+                g.tensor.wait_ge(S[name], val)
+
+        for i, (q, s) in enumerate(seq):
+            tile, t_sem, t_val = operand(q, s)
+            if s == 2:
+                twait("s_c2", NE)
+                rhs = y(2)
+            elif s == 5:
+                twait("s_c5", NE)
+                rhs = T.c5[:, :]
             else:
-                g.tensor.wait_ge(land[q][1], NE)
-            for s in range(2, q):
-                if q == r:
-                    tile = T.own[:, _col(s):_col(s + 1)]
-                else:
-                    tile = land[q][0][:, P * (s - 2):P * (s - 1)]
-                if s == q - 1 and s >= 3:
-                    g.tensor.wait_ge(yvs[s], 1)
-                mm = g.tensor.matmul(ps[q][:, 0:K], tile, y(s), s == 2, s == q - 1)
-            mm.then_inc(mms[q], 1)
+                twait("yv%d" % s, 1)
+                rhs = y(s)
+            twait(t_sem, t_val)
+            first = q not in [a for a, _b in seq[:i]]
+            last = q not in [a for a, _b in seq[i + 1:]]
+            mm = g.tensor.matmul(ps[q][:, 0:K], tile, rhs, first, last)
+            if last:
+                mm.then_inc(mms[q], 1)
+        for q in rows:
             c_ap, c_sem, c_val = cs[q]
             g.vector.wait_ge(c_sem, c_val)
             g.vector.wait_ge(mms[q], 1)
-            g.vector.tensor_tensor(y(q), c_ap, ps[q][:, 0:K], AluOpType.subtract).then_inc(yvs[q], 1)
+            g.vector.tensor_tensor(y(q), c_ap, ps[q][:, 0:K], SUB).then_inc(yvs[q], 1)
         store(y(r), yvs[r])
 
     if core == R[0]:
@@ -152,9 +200,9 @@ def rank_program(g, core, T, topo):
         if mine:
             load_b_part(1)
             g.wait_ge(S.ldB, 32)
-            send(T.own[:, 0:_col(1)], T.own[:, 0:_col(1)], [H1], S.s_row)
+            send(T.own[:, 0:_col(1)], T.own[:, 0:_col(1)], [H1], S.s_row1)
         g.tensor.wait_ge(S.s_b0, NE)
-        partial(T.own, S.ldB if mine else S.s_row, 32 if mine else NE, T.psc, T.y01[:, K:2 * K], S.mmc, ntiles=1)
+        partial(T.own, S.ldB if mine else S.s_row1, 32 if mine else NE, T.psc, T.y01[:, K:2 * K], S.mmc, ntiles=1)
         if mine:
             store(T.y01[:, K:2 * K], S.cv)
         g.wait_ge(S.s_b0, NE)
@@ -194,21 +242,34 @@ def rank_program(g, core, T, topo):
         load_a_part(4)
         load_b_part(2)
         g.wait_ge(S.ldA, 16)
-        send(T.own[:, _col(2):_col(4)], T.own[:, _col(2):_col(4)], [H4a, H4b], S.s_rowA)
+        send_each(T.own[:, _col(2):_col(4)], T.own[:, _col(2):_col(4)], [H4a, H4b], S.s_rowA)
         g.wait_ge(S.ldB, 32)
-        send(T.own[:, 0:_col(2)], T.own[:, 0:_col(2)], [H4a, H4b], S.s_row)
+        send_each(T.own[:, 0:_col(2)], T.own[:, 0:_col(2)], [H4a, H4b], S.s_row)
         solve_group(4)
         finish(True)
 
     elif core in (H4a, H4b):
         first = core == H4a
+        lo = 3 if FOLD42 else 2
         g.wait_ge(S.s_rowA, NE)
-        send(T.own[:, _col(2):_col(4)], T.a4x[:, :], [R[6] if first else R[5]], S.s_a4x)
+        send(T.own[:, _col(lo):_col(4)], T.a4x[:, P * (lo - 2):2 * P], [R[6] if first else R[5]], S.s_a4x)
         g.tensor.wait_ge(S.s_y01, NE)
         partial(T.row2, S.s_row2, NE, T.psc, T.c24[:, 0:K], S.mmc)
-        partial(T.own, S.s_row, NE, T.ps4, T.c24[:, K:2 * K], S.mm4)
-        g.wait_ge(S.cv, 2)
-        send(T.c24[:, :], T.c24[:, :], [R[6], R[4]] if first else [R[5], R[3]], S.s_c24)
+        g.tensor.wait_ge(S.s_row, NE)
+        g.tensor.matmul(T.ps4[:, 0:K], T.own[:, _col(0):_col(1)], T.y01[:, 0:K], True, False)
+        mm = g.tensor.matmul(T.ps4[:, 0:K], T.own[:, _col(1):_col(2)], T.y01[:, K:2 * K], False, not FOLD42)
+        if FOLD42:
+            g.tensor.wait_ge(S.s_rowA, NE)
+            g.tensor.wait_ge(S.cv, 1)
+            mm = g.tensor.matmul(T.ps4[:, 0:K], T.own[:, _col(2):_col(3)], T.c24[:, 0:K], False, True)
+        mm.then_inc(S.mm4, 1)
+        g.vector.wait_ge(S.s_row, NE)
+        g.vector.wait_ge(S.mm4, 1)
+        g.vector.tensor_tensor(T.c24[:, K:2 * K], T.own[:, 0:K], T.ps4[:, 0:K], SUB).then_inc(S.cv2, 1)
+        g.wait_ge(S.cv, 1)
+        send(T.c24[:, 0:K], T.c24[:, 0:K], [R[6], R[4]] if first else [R[5], R[3]], S.s_c2)
+        g.wait_ge(S.cv2, 1)
+        send(T.c24[:, K:2 * K], T.c24[:, K:2 * K], [R[6], R[4]] if first else [R[5]], S.s_c4)
         finish(False)
 
     elif core == R[5]:
@@ -226,6 +287,26 @@ def rank_program(g, core, T, topo):
     elif core == R[6]:
         load_b_part(2)
         load_a_part(6)
+        g.vector.memset(T.eye_src[:, 1:P + 1], 0.0).then_inc(S.ms, 1)
+        g.vector.memset(T.eye_src[:, 0:1], 1.0).then_inc(S.ms, 1)
+        g.scalar.wait_ge(S.ms, 2)
+        g.scalar.dma_start(T.eye_d[:, :], T.eye_src[:, :]).then_inc(S.ed, 16)
+        g.scalar.wait_ge(S.ed, 16)
+        g.scalar.dma_start(T.eye[:, :], T.eye_d[0:P, :]).then_inc(S.ed2, 16)
+        g.tensor.wait_ge(S.ed2, 16)
+        g.tensor.wait_ge(S.s_a5x, NE)
+        for j in range(3):
+            g.tensor.matmul(T.pt[:, P * j:P * (j + 1)], T.a5x[:, P * j:P * (j + 1)], T.eye[:, :], True, True).then_inc(S.tp, 1)
+        g.vector.wait_ge(S.tp, 3)
+        g.vector.tensor_copy(T.t5[:, :], T.pt[:, 0:3 * P]).then_inc(S.tc, 1)
+        g.tensor.wait_ge(S.tc, 1)
+        g.tensor.wait_ge(S.ldA, 16)
+        for j in range(3):
+            g.tensor.matmul(T.pu[:, P * j:P * (j + 1)], T.t5[:, P * j:P * (j + 1)], T.own[:, _col(5):_col(6)],
+                            True, True).then_inc(S.up, 1)
+        g.vector.wait_ge(S.up, 3)
+        g.vector.wait_ge(S.ldA, 16)
+        g.vector.tensor_tensor(T.u6[:, :], T.own[:, _col(2):_col(5)], T.pu[:, 0:3 * P], SUB).then_inc(S.uc, 1)
         g.tensor.wait_ge(S.s_y01, NE)
         partial(T.own, S.ldB, 32, T.psc, T.c6[:, :], S.mmc)
         solve_group(6)

@@ -4,7 +4,8 @@ from concourse.mybir import AluOpType
 P = 128
 K = 64
 NT = 6
-FOLD42 = True
+NE = 8
+NC = 16
 
 
 def _col(s):
@@ -13,35 +14,31 @@ def _col(s):
 
 SCRATCH = {
     "own": ("sbuf", [P, K + NT * P], "float32"),
-    "row2": ("sbuf", [P, K + 2 * P], "float32"),
     "y01": ("sbuf", [P, 2 * K], "float32"),
     "c24": ("sbuf", [P, 2 * K], "float32"),
     "c3": ("sbuf", [P, K], "float32"),
     "c5": ("sbuf", [P, K], "float32"),
-    "c6": ("sbuf", [P, K], "float32"),
-    "a32": ("sbuf", [P, P], "float32"),
-    "a4x": ("sbuf", [P, 2 * P], "float32"),
-    "a5x": ("sbuf", [P, 3 * P], "float32"),
-    "yy": ("sbuf", [P, 4 * K], "float32"),
-    "eye_src": ("sbuf", [P, P + 1], "float32"),
-    "eye_d": ("dram", [P + 1, P], "float32"),
+    "a32t": ("sbuf", [P, P], "float32"),
+    "a4t": ("sbuf", [P, 2 * P], "float32"),
+    "a5t": ("sbuf", [P, 3 * P], "float32"),
+    "ones": ("sbuf", [P, P], "float32"),
     "eye": ("sbuf", [P, P], "float32"),
-    "t5": ("sbuf", [P, 3 * P], "float32"),
-    "u6": ("sbuf", [P, 3 * P], "float32"),
+    "tt": ("sbuf", [P, 3 * P], "float32"),
+    "v": ("sbuf", [P, 3 * P], "float32"),
+    "yy": ("sbuf", [P, K], "float32"),
     "psc": ("psum", [P, 512], "float32"),
-    "ps3": ("psum", [P, 512], "float32"),
-    "ps4": ("psum", [P, 512], "float32"),
-    "ps5": ("psum", [P, 512], "float32"),
-    "ps6": ("psum", [P, 512], "float32"),
-    "pt": ("psum", [P, 512], "float32"),
-    "pu": ("psum", [P, 512], "float32"),
+    "pt0": ("psum", [P, 512], "float32"),
+    "pt1": ("psum", [P, 512], "float32"),
+    "pt2": ("psum", [P, 512], "float32"),
+    "pv2": ("psum", [P, 512], "float32"),
+    "pv3": ("psum", [P, 512], "float32"),
+    "pf": ("psum", [P, 512], "float32"),
 }
-SEMAPHORES = ["ldA", "ldB", "st", "sent",
-              "s_b0", "s_row1", "s_row", "s_rowA", "s_row2", "s_y01", "s_a32", "s_a4x", "s_a5x", "s_c3", "s_c5", "s_c2",
-              "s_c4", "mmc", "cv", "cv2", "mm3", "mm4", "mm5", "mm6", "yv3", "yv4", "yv5", "yv6",
-              "ms", "ed", "ed2", "tp", "tc", "up", "uc"]
-
-NE = 8
+SEMAPHORES = ["ldA", "ldB", "ld2", "ld3", "ld4", "st", "sent",
+              "s_b0", "s_y1", "s_row", "s_rowA", "s_a32", "s_a42", "s_a43", "s_a52", "s_a53", "s_a54",
+              "s_c2", "s_c3", "s_c4", "s_c5",
+              "mmc", "cv", "mmf", "yv", "ms", "ey", "tp2", "tp3", "tp4", "tc2", "tc3", "tc4",
+              "vm2", "vm3", "vm4", "vv2", "vv3", "vv4"]
 
 
 def _low_bits(mask, n):
@@ -64,14 +61,27 @@ def _helpers(c, T, topo):
 
 def rank_program(g, core, T, topo):
     R = list(T.cores)
+    H0 = _helpers(R[0], T, topo)[0]
     H1 = _helpers(R[1], T, topo)[0]
     H3 = _helpers(R[3], T, topo)[0]
     H4a, H4b = _helpers(R[4], T, topo)[0:2]
-    if core not in R and core not in (H1, H3, H4a, H4b):
+    if core not in R and core not in (H0, H1, H3, H4a, H4b):
         return
     S = T.sem
     sent = [0]
     SUB = AluOpType.subtract
+    tseen, vseen = [], []
+    own_sems = [("ldA", 16)]
+
+    def twait(name, val):
+        if (name, val) not in tseen:
+            tseen.append((name, val))
+            g.tensor.wait_ge(S[name], val)
+
+    def vwait(name, val):
+        if (name, val) not in vseen:
+            vseen.append((name, val))
+            g.vector.wait_ge(S[name], val)
 
     def common_mask(dsts):
         mask = topo.mask(core, dsts[0])
@@ -82,27 +92,16 @@ def rank_program(g, core, T, topo):
     def dst_id(d):
         return DstId(rid=topo.addr(d)[0], pnc=topo.addr(d)[1])
 
-    def send(src, dst, dsts, sem):
-        mask = _low_bits(common_mask(dsts), NE)
-        if len(dsts) == 1:
-            rid, pid, _se = topo.addr(dsts[0])
-            g.remote_dma(out_ap=dst, in_ap=src, remote_sem=sem, local_sem=S.sent, pid=pid, routing_id=rid,
-                         dma_engine_mask=mask)
-        else:
-            g.remote_dma_fused([RemoteDMATransfer(dst_ids=[dst_id(d) for d in dsts], dma_engine_mask=mask, remote_sem=sem,
-                                                  srcs=[src], dsts=[dst for _d in dsts], alu_op=0)], local_sem=S.sent)
-        sent[0] += NE
-
-    def send_each(src, dst, dsts, sem):
+    def transfer(src, dst, dsts, sem, beside=None, ne=NE):
         mask = common_mask(dsts)
-        trs = []
-        for d in dsts:
-            part = _low_bits(mask, NE)
-            mask &= ~part
-            trs.append(RemoteDMATransfer(dst_ids=[dst_id(d)], dma_engine_mask=part, remote_sem=sem, srcs=[src],
-                                         dsts=[dst], alu_op=0))
-            sent[0] += NE
-        g.remote_dma_fused(trs, local_sem=S.sent)
+        if beside is not None:
+            mask &= ~topo.mask(core, beside)
+        sent[0] += ne
+        return RemoteDMATransfer(dst_ids=[dst_id(d) for d in dsts], dma_engine_mask=_low_bits(mask, ne), remote_sem=sem,
+                                 srcs=[src], dsts=[dst for _d in dsts], alu_op=0)
+
+    def send(src, dst, dsts, sem, beside=None, ne=NE):
+        g.remote_dma_fused([transfer(src, dst, dsts, sem, beside, ne)], local_sem=S.sent)
 
     def finish(stored):
         if sent[0]:
@@ -121,193 +120,190 @@ def rank_program(g, core, T, topo):
     def load_a_part(r):
         g.sync.dma_start(T.own[:, _col(2):_col(r)], T.l[:, P * 2:P * r]).then_inc(S.ldA, 16)
 
-    def partial(row, row_sem, row_val, ps, out, mm_sem, ntiles=2):
-        g.tensor.wait_ge(row_sem, row_val)
-        for s in range(ntiles):
-            mm = g.tensor.matmul(ps[:, 0:K], row[:, _col(s):_col(s + 1)], T.y01[:, K * s:K * (s + 1)],
-                                 s == 0, s == ntiles - 1)
-        mm.then_inc(mm_sem, 1)
-        g.vector.wait_ge(row_sem, row_val)
-        g.vector.wait_ge(mm_sem, 1)
-        g.vector.tensor_tensor(out, row[:, 0:K], ps[:, 0:K], SUB).then_inc(S.cv, 1)
+    def tile(s):
+        return T.own[:, _col(s):_col(s + 1)]
 
-    def solve_group(r):
-        ps = {3: T.ps3, 4: T.ps4, 5: T.ps5, 6: T.ps6}
-        mms = {3: S.mm3, 4: S.mm4, 5: S.mm5, 6: S.mm6}
-        yvs = {3: S.yv3, 4: S.yv4, 5: S.yv5, 6: S.yv6}
-        cs = {3: (T.c3[:, :], S.s_c3, NE), 4: (T.c24[:, K:2 * K], S.s_c4, NE), 5: (T.c5[:, :], S.cv, 1),
-              6: (T.c6[:, :], S.cv, 1)}
+    Y0, Y1 = T.y01[:, 0:K], T.y01[:, K:2 * K]
+    C2, C4 = T.c24[:, 0:K], T.c24[:, K:2 * K]
+    B_PART = T.own[:, 0:_col(2)]
 
-        def y(s):
-            return T.c24[:, 0:K] if s == 2 else T.yy[:, K * (s - 3):K * (s - 2)]
+    def group01(ps, row_name, row_val, ntiles, stop):
+        twait(row_name, row_val)
+        twait("s_b0", NE)
+        mm = g.tensor.matmul(ps[:, 0:K], tile(0), Y0, True, stop and ntiles == 1)
+        if ntiles == 2:
+            twait("s_y1", NE)
+            mm = g.tensor.matmul(ps[:, 0:K], tile(1), Y1, False, stop)
+        return mm
 
-        def operand(q, s):
-            if q == 6 and s < 5:
-                return T.u6[:, P * (s - 2):P * (s - 1)], "uc", 1
-            if q == r:
-                return T.own[:, _col(s):_col(s + 1)], "ldA", 16
-            if q == 3:
-                return T.a32[:, :], "s_a32", NE
-            return T.a4x[:, P * (s - 2):P * (s - 1)], "s_a4x", NE
+    def partial(row_name, row_val, out, ntiles=2):
+        group01(T.psc, row_name, row_val, ntiles, True).then_inc(S.mmc, 1)
+        vwait(row_name, row_val)
+        vwait("mmc", 1)
+        g.vector.tensor_tensor(out, T.own[:, 0:K], T.psc[:, 0:K], SUB).then_inc(S.cv, 1)
 
-        if FOLD42:
-            seq = [(3, 2), (r, 2), (4, 3), (r, 3), (r, 5), (r, 4)]
-        else:
-            seq = [(3, 2), (4, 2), (4, 3), (r, 2), (r, 3), (r, 5), (r, 4)]
-        seq = [(q, s) for i, (q, s) in enumerate(seq) if q <= r and s < q and (q, s) not in seq[:i]
-               and not (FOLD42 and (q, s) == (4, 2))]
-        rows = [q for q in (3, 4, 5, 6) if q <= min(r, 4) or q == r]
-        seen = []
+    def make_eye():
+        g.vector.memset(T.ones[:, :], 1.0).then_inc(S.ms, 1)
+        g.wait_ge(S.ms, 1)
+        g.affine_select(T.eye[:, :], T.ones[:, :], [[-1, P]], AluOpType.is_equal, 0.0, 0, 1).then_inc(S.ey, 1)
 
-        def twait(name, val):
-            if name not in seen:
-                seen.append(name)
-                g.tensor.wait_ge(S[name], val)
+    def turn_and_send(tiles, waits, buf, q, dsts):
+        pts = {2: T.pt2, 3: T.pt1, 4: T.pt0}
+        twait("ey", 1)
+        for s, (name, val) in zip(tiles, waits):
+            twait(name, val)
+            g.tensor.matmul(pts[s][:, 0:P], tile(s), T.eye[:, :], True, True).then_inc(S["tp%d" % s], 1)
+        for s in tiles:
+            vwait("tp%d" % s, 1)
+            g.vector.tensor_copy(T.tt[:, P * (s - 2):P * (s - 1)], pts[s][:, 0:P]).then_inc(S["tc%d" % s], 1)
+        for s in tiles:
+            g.wait_ge(S["tc%d" % s], 1)
+            send(T.tt[:, P * (s - 2):P * (s - 1)], buf[:, P * (s - 2):P * (s - 1)], dsts, S["s_a%d%d" % (q, s)])
 
-        for i, (q, s) in enumerate(seq):
-            tile, t_sem, t_val = operand(q, s)
-            if s == 2:
-                twait("s_c2", NE)
-                rhs = y(2)
-            elif s == 5:
-                twait("s_c5", NE)
-                rhs = T.c5[:, :]
+    def v_t(s):
+        return T.v[:, P * (s - 2):P * (s - 1)]
+
+    def eliminate(r, after_first=None):
+        pv = {2: T.pv2, 3: T.pv3, 4: T.pt0}
+        at = {5: T.a5t, 4: T.a4t, 3: T.a32t}
+        for q in range(r - 1, 2, -1):
+            if q == r - 1:
+                for name, val in own_sems:
+                    twait(name, val)
+                rhs = tile(q)
             else:
-                twait("yv%d" % s, 1)
-                rhs = y(s)
-            twait(t_sem, t_val)
-            first = q not in [a for a, _b in seq[:i]]
-            last = q not in [a for a, _b in seq[i + 1:]]
-            mm = g.tensor.matmul(ps[q][:, 0:K], tile, rhs, first, last)
-            if last:
-                mm.then_inc(mms[q], 1)
-        for q in rows:
-            c_ap, c_sem, c_val = cs[q]
-            g.vector.wait_ge(c_sem, c_val)
-            g.vector.wait_ge(mms[q], 1)
-            g.vector.tensor_tensor(y(q), c_ap, ps[q][:, 0:K], SUB).then_inc(yvs[q], 1)
-        store(y(r), yvs[r])
+                twait("vv%d" % q, 1)
+                rhs = v_t(q)
+            for s in range(q - 1, 1, -1):
+                twait("s_a%d%d" % (q, s), NE)
+                mm = g.tensor.matmul(pv[s][:, 0:P], at[q][:, P * (s - 2):P * (s - 1)], rhs, q == r - 1, q == s + 1)
+                if q == s + 1:
+                    mm.then_inc(S["vm%d" % s], 1)
+            s = q - 1
+            for name, val in own_sems:
+                vwait(name, val)
+            vwait("vm%d" % s, 1)
+            g.vector.tensor_tensor(v_t(s), tile(s), pv[s][:, 0:P], SUB).then_inc(S["vv%d" % s], 1)
+            if q == r - 1 and after_first is not None:
+                after_first()
+
+    def last_group(terms, opened, c_ap, c_name, c_val):
+        for i, (lhs, rhs, waits) in enumerate(terms):
+            for name, val in waits:
+                twait(name, val)
+            mm = g.tensor.matmul(T.pf[:, 0:K], lhs, rhs, i == 0 and not opened, i == len(terms) - 1)
+        mm.then_inc(S.mmf, 1)
+        vwait(c_name, c_val)
+        vwait("mmf", 1)
+        g.vector.tensor_tensor(T.yy[:, :], c_ap, T.pf[:, 0:K], SUB).then_inc(S.yv, 1)
+        store(T.yy[:, :], S.yv)
 
     if core == R[0]:
         g.sync.dma_start(T.own[:, 0:K], T.b[:, :]).then_inc(S.ldB, 16)
         g.scalar.dma_start(T.y[:, :], T.b[:, :]).then_inc(S.st, 16)
         g.wait_ge(S.ldB, 16)
-        send(T.own[:, 0:K], T.y01[:, 0:K], [H1, R[1]], S.s_b0)
+        g.remote_dma_fused([transfer(T.own[:, 0:K], Y0, [H1, R[1], H3, R[5], R[6]], S.s_b0),
+                            transfer(T.own[:, 0:K], Y0, [H0], S.s_b0, beside=H1)], local_sem=S.sent)
         finish(True)
+
+    elif core == H0:
+        g.wait_ge(S.s_b0, NE)
+        send(Y0, Y0, [H4a, H4b, R[2]], S.s_b0)
+        finish(False)
 
     elif core in (R[1], H1):
         mine = core == R[1]
         if mine:
             load_b_part(1)
             g.wait_ge(S.ldB, 32)
-            send(T.own[:, 0:_col(1)], T.own[:, 0:_col(1)], [H1], S.s_row1)
-        g.tensor.wait_ge(S.s_b0, NE)
-        partial(T.own, S.ldB if mine else S.s_row1, 32 if mine else NE, T.psc, T.y01[:, K:2 * K], S.mmc, ntiles=1)
+            send(T.own[:, 0:_col(1)], T.own[:, 0:_col(1)], [H1], S.s_row, ne=NC)
+        partial("ldB" if mine else "s_row", 32 if mine else NC, Y1, ntiles=1)
         if mine:
-            store(T.y01[:, K:2 * K], S.cv)
-        g.wait_ge(S.s_b0, NE)
+            store(Y1, S.cv)
         g.wait_ge(S.cv, 1)
-        send(T.y01[:, :], T.y01[:, :], [H3, R[5], R[6]] if mine else [H4a, H4b, R[2]], S.s_y01)
+        send(Y1, Y1, [H3, R[5], R[6]] if mine else [H4a, H4b, R[2]], S.s_y1)
         finish(mine)
 
     elif core == R[2]:
         load_b_part(2)
         g.wait_ge(S.ldB, 32)
-        send(T.own[:, 0:_col(2)], T.row2[:, :], [H4a, H4b], S.s_row2)
-        g.tensor.wait_ge(S.s_y01, NE)
-        partial(T.own, S.ldB, 32, T.psc, T.yy[:, 0:K], S.mmc)
-        store(T.yy[:, 0:K], S.cv)
+        send(B_PART, B_PART, [H4a], S.s_row)
+        partial("ldB", 32, T.yy[:, :])
+        store(T.yy[:, :], S.cv)
         finish(True)
 
     elif core == R[3]:
-        load_b_part(2)
+        make_eye()
         load_a_part(3)
+        load_b_part(2)
         g.wait_ge(S.ldB, 32)
-        g.wait_ge(S.ldA, 16)
-        send(T.own[:, 0:_col(3)], T.own[:, 0:_col(3)], [H3], S.s_row)
-        send(T.own[:, _col(2):_col(3)], T.a32[:, :], [R[6], R[5]], S.s_a32)
-        solve_group(3)
+        send(B_PART, B_PART, [H3], S.s_row, ne=NC)
+        turn_and_send([2], [("ldA", 16)], T.a32t, 3, [H3, R[6], R[5]])
+        last_group([(tile(2), C2, [("ldA", 16), ("s_c2", NE)])], False, T.c3[:, :], "s_c3", NE)
         finish(True)
 
     elif core == H3:
-        g.wait_ge(S.s_row, NE)
-        send(T.own[:, _col(2):_col(3)], T.a32[:, :], [R[4]], S.s_a32)
-        g.tensor.wait_ge(S.s_y01, NE)
-        partial(T.own, S.s_row, NE, T.psc, T.c3[:, :], S.mmc)
+        g.wait_ge(S.s_a32, NE)
+        send(T.a32t[:, :], T.a32t[:, :], [R[4]], S.s_a32)
+        partial("s_row", NC, T.c3[:, :])
         g.wait_ge(S.cv, 1)
-        send(T.c3[:, :], T.c3[:, :], [R[4], R[6], R[5], R[3]], S.s_c3)
+        send(T.c3[:, :], T.c3[:, :], [R[4], R[6], R[5]], S.s_c3)
+        send(T.c3[:, :], T.c3[:, :], [R[3]], S.s_c3, beside=R[4])
         finish(False)
 
     elif core == R[4]:
         load_a_part(4)
         load_b_part(2)
         g.wait_ge(S.ldA, 16)
-        send_each(T.own[:, _col(2):_col(4)], T.own[:, _col(2):_col(4)], [H4a, H4b], S.s_rowA)
+        g.remote_dma_fused([transfer(tile(3), tile(3), [H4a], S.s_rowA),
+                            transfer(tile(2), tile(2), [H4b], S.s_rowA, beside=R[2])], local_sem=S.sent)
         g.wait_ge(S.ldB, 32)
-        send_each(T.own[:, 0:_col(2)], T.own[:, 0:_col(2)], [H4a, H4b], S.s_row)
-        solve_group(4)
+        send(B_PART, B_PART, [H4b], S.s_row, ne=NC)
+        eliminate(4)
+        last_group([(tile(3), T.c3[:, :], [("s_c3", NE)]),
+                    (v_t(2), C2, [("s_c2", NE), ("vv2", 1)])], False, C4, "s_c4", NE)
         finish(True)
 
-    elif core in (H4a, H4b):
-        first = core == H4a
-        lo = 3 if FOLD42 else 2
-        g.wait_ge(S.s_rowA, NE)
-        send(T.own[:, _col(lo):_col(4)], T.a4x[:, P * (lo - 2):2 * P], [R[6] if first else R[5]], S.s_a4x)
-        g.tensor.wait_ge(S.s_y01, NE)
-        partial(T.row2, S.s_row2, NE, T.psc, T.c24[:, 0:K], S.mmc)
-        g.tensor.wait_ge(S.s_row, NE)
-        g.tensor.matmul(T.ps4[:, 0:K], T.own[:, _col(0):_col(1)], T.y01[:, 0:K], True, False)
-        mm = g.tensor.matmul(T.ps4[:, 0:K], T.own[:, _col(1):_col(2)], T.y01[:, K:2 * K], False, not FOLD42)
-        if FOLD42:
-            g.tensor.wait_ge(S.s_rowA, NE)
-            g.tensor.wait_ge(S.cv, 1)
-            mm = g.tensor.matmul(T.ps4[:, 0:K], T.own[:, _col(2):_col(3)], T.c24[:, 0:K], False, True)
-        mm.then_inc(S.mm4, 1)
-        g.vector.wait_ge(S.s_row, NE)
-        g.vector.wait_ge(S.mm4, 1)
-        g.vector.tensor_tensor(T.c24[:, K:2 * K], T.own[:, 0:K], T.ps4[:, 0:K], SUB).then_inc(S.cv2, 1)
+    elif core == H4a:
+        make_eye()
+        turn_and_send([3], [("s_rowA", NE)], T.a4t, 4, [R[6], R[5]])
+        partial("s_row", NE, C2)
         g.wait_ge(S.cv, 1)
-        send(T.c24[:, 0:K], T.c24[:, 0:K], [R[6], R[4]] if first else [R[5], R[3]], S.s_c2)
-        g.wait_ge(S.cv2, 1)
-        send(T.c24[:, K:2 * K], T.c24[:, K:2 * K], [R[6], R[4]] if first else [R[5]], S.s_c4)
+        send(C2, C2, [R[6], R[5], R[3]], S.s_c2)
+        send(C2, C2, [R[4]], S.s_c2, beside=R[6])
+        finish(False)
+
+    elif core == H4b:
+        make_eye()
+        turn_and_send([2], [("s_rowA", NE)], T.a4t, 4, [R[6], R[5]])
+        partial("s_row", NC, C4)
+        g.wait_ge(S.cv, 1)
+        send(C4, C4, [R[6], R[5]], S.s_c4)
+        send(C4, C4, [R[4]], S.s_c4, beside=R[6])
         finish(False)
 
     elif core == R[5]:
-        load_a_part(5)
+        make_eye()
+        own_sems[:] = [("ld%d" % s, 16) for s in (4, 3, 2)]
+        for s in (4, 3, 2):
+            g.sync.dma_start(tile(s), T.l[:, P * s:P * (s + 1)]).then_inc(S["ld%d" % s], 16)
         load_b_part(2)
-        g.wait_ge(S.ldA, 16)
-        send(T.own[:, _col(2):_col(5)], T.a5x[:, :], [R[6]], S.s_a5x)
-        g.tensor.wait_ge(S.s_y01, NE)
-        partial(T.own, S.ldB, 32, T.psc, T.c5[:, :], S.mmc)
+        turn_and_send([4, 3, 2], own_sems, T.a5t, 5, [R[6]])
+        partial("ldB", 32, T.c5[:, :])
         g.wait_ge(S.cv, 1)
         send(T.c5[:, :], T.c5[:, :], [R[6]], S.s_c5)
-        solve_group(5)
+        eliminate(5)
+        last_group([(v_t(3), T.c3[:, :], [("s_c3", NE), ("vv3", 1)]),
+                    (v_t(2), C2, [("s_c2", NE), ("vv2", 1)]),
+                    (tile(4), C4, [("s_c4", NE)])], False, T.c5[:, :], "cv", 1)
         finish(True)
 
     elif core == R[6]:
-        load_b_part(2)
         load_a_part(6)
-        g.vector.memset(T.eye_src[:, 1:P + 1], 0.0).then_inc(S.ms, 1)
-        g.vector.memset(T.eye_src[:, 0:1], 1.0).then_inc(S.ms, 1)
-        g.scalar.wait_ge(S.ms, 2)
-        g.scalar.dma_start(T.eye_d[:, :], T.eye_src[:, :]).then_inc(S.ed, 16)
-        g.scalar.wait_ge(S.ed, 16)
-        g.scalar.dma_start(T.eye[:, :], T.eye_d[0:P, :]).then_inc(S.ed2, 16)
-        g.tensor.wait_ge(S.ed2, 16)
-        g.tensor.wait_ge(S.s_a5x, NE)
-        for j in range(3):
-            g.tensor.matmul(T.pt[:, P * j:P * (j + 1)], T.a5x[:, P * j:P * (j + 1)], T.eye[:, :], True, True).then_inc(S.tp, 1)
-        g.vector.wait_ge(S.tp, 3)
-        g.vector.tensor_copy(T.t5[:, :], T.pt[:, 0:3 * P]).then_inc(S.tc, 1)
-        g.tensor.wait_ge(S.tc, 1)
-        g.tensor.wait_ge(S.ldA, 16)
-        for j in range(3):
-            g.tensor.matmul(T.pu[:, P * j:P * (j + 1)], T.t5[:, P * j:P * (j + 1)], T.own[:, _col(5):_col(6)],
-                            True, True).then_inc(S.up, 1)
-        g.vector.wait_ge(S.up, 3)
-        g.vector.wait_ge(S.ldA, 16)
-        g.vector.tensor_tensor(T.u6[:, :], T.own[:, _col(2):_col(5)], T.pu[:, 0:3 * P], SUB).then_inc(S.uc, 1)
-        g.tensor.wait_ge(S.s_y01, NE)
-        partial(T.own, S.ldB, 32, T.psc, T.c6[:, :], S.mmc)
-        solve_group(6)
+        load_b_part(2)
+        eliminate(6, lambda: group01(T.pf, "ldB", 32, 2, False))
+        last_group([(tile(5), T.c5[:, :], [("s_c5", NE)]),
+                    (v_t(3), T.c3[:, :], [("s_c3", NE), ("vv3", 1)]),
+                    (v_t(2), C2, [("s_c2", NE), ("vv2", 1)]),
+                    (v_t(4), C4, [("s_c4", NE), ("vv4", 1)])], True, T.own[:, 0:K], "ldB", 32)
         finish(True)

from concourse.bass import DstId, RemoteDMATransfer
from concourse.mybir import AluOpType

P = 128
K = 64
NT = 6
NE = 8
NC = 16


def _col(s):
    return K + P * s


SCRATCH = {
    "own": ("sbuf", [P, K + NT * P], "float32"),
    "y01": ("sbuf", [P, 2 * K], "float32"),
    "c24": ("sbuf", [P, 2 * K], "float32"),
    "c3": ("sbuf", [P, K], "float32"),
    "c5": ("sbuf", [P, K], "float32"),
    "a32t": ("sbuf", [P, P], "float32"),
    "a4t": ("sbuf", [P, 2 * P], "float32"),
    "a5t": ("sbuf", [P, 3 * P], "float32"),
    "ones": ("sbuf", [P, P], "float32"),
    "eye": ("sbuf", [P, P], "float32"),
    "tt": ("sbuf", [P, 3 * P], "float32"),
    "v": ("sbuf", [P, 3 * P], "float32"),
    "yy": ("sbuf", [P, K], "float32"),
    "psc": ("psum", [P, 512], "float32"),
    "pt0": ("psum", [P, 512], "float32"),
    "pt1": ("psum", [P, 512], "float32"),
    "pt2": ("psum", [P, 512], "float32"),
    "pv2": ("psum", [P, 512], "float32"),
    "pv3": ("psum", [P, 512], "float32"),
    "pf": ("psum", [P, 512], "float32"),
}
SEMAPHORES = ["ldA", "ldB", "ld2", "ld3", "ld4", "st", "sent",
              "s_b0", "s_y1", "s_row", "s_rowA", "s_a32", "s_a42", "s_a43", "s_a52", "s_a53", "s_a54",
              "s_c2", "s_c3", "s_c4", "s_c5",
              "mmc", "cv", "mmf", "yv", "ms", "ey", "tp2", "tp3", "tp4", "tc2", "tc3", "tc4",
              "vm2", "vm3", "vm4", "vv2", "vv3", "vv4"]


def _low_bits(mask, n):
    out, got, bit = 0, 0, 1
    while got < n:
        if mask & bit:
            out |= bit
            got += 1
        bit <<= 1
    return out


def _helpers(c, T, topo):
    far = [x for x in T.cores
           if topo.chip(x) != topo.chip(c) and not topo.same_plane(topo.chip(x), topo.chip(c))]
    return [h for h in range(topo.CHIPS * topo.CORES_PER_CHIP)
            if topo.chip(h) == topo.chip(c) and topo.die(h) == topo.die(c) and h not in T.cores
            and all(topo.may_write(h, x) for x in far)]


def rank_program(g, core, T, topo):
    R = list(T.cores)
    H0 = _helpers(R[0], T, topo)[0]
    H1 = _helpers(R[1], T, topo)[0]
    H3 = _helpers(R[3], T, topo)[0]
    H4a, H4b = _helpers(R[4], T, topo)[0:2]
    if core not in R and core not in (H0, H1, H3, H4a, H4b):
        return
    S = T.sem
    sent = [0]
    SUB = AluOpType.subtract
    tseen, vseen = [], []
    own_sems = [("ldA", 16)]

    def twait(name, val):
        if (name, val) not in tseen:
            tseen.append((name, val))
            g.tensor.wait_ge(S[name], val)

    def vwait(name, val):
        if (name, val) not in vseen:
            vseen.append((name, val))
            g.vector.wait_ge(S[name], val)

    def common_mask(dsts):
        mask = topo.mask(core, dsts[0])
        for d in dsts:
            mask &= topo.mask(core, d)
        return mask

    def dst_id(d):
        return DstId(rid=topo.addr(d)[0], pnc=topo.addr(d)[1])

    def transfer(src, dst, dsts, sem, beside=None, ne=NE):
        mask = common_mask(dsts)
        if beside is not None:
            mask &= ~topo.mask(core, beside)
        sent[0] += ne
        return RemoteDMATransfer(dst_ids=[dst_id(d) for d in dsts], dma_engine_mask=_low_bits(mask, ne), remote_sem=sem,
                                 srcs=[src], dsts=[dst for _d in dsts], alu_op=0)

    def send(src, dst, dsts, sem, beside=None, ne=NE):
        g.remote_dma_fused([transfer(src, dst, dsts, sem, beside, ne)], local_sem=S.sent)

    def finish(stored):
        if sent[0]:
            g.wait_ge(S.sent, sent[0])
        if stored:
            g.wait_ge(S.st, 16)

    def store(src, sem):
        g.sync.wait_ge(sem, 1)
        g.sync.dma_start(T.y[:, :], src).then_inc(S.st, 16)

    def load_b_part(ntiles):
        g.sync.dma_start(T.own[:, 0:K], T.b[:, :]).then_inc(S.ldB, 16)
        g.scalar.dma_start(T.own[:, K:_col(ntiles)], T.l[:, 0:P * ntiles]).then_inc(S.ldB, 16)

    def load_a_part(r):
        g.sync.dma_start(T.own[:, _col(2):_col(r)], T.l[:, P * 2:P * r]).then_inc(S.ldA, 16)

    def tile(s):
        return T.own[:, _col(s):_col(s + 1)]

    Y0, Y1 = T.y01[:, 0:K], T.y01[:, K:2 * K]
    C2, C4 = T.c24[:, 0:K], T.c24[:, K:2 * K]
    B_PART = T.own[:, 0:_col(2)]

    def group01(ps, row_name, row_val, ntiles, stop):
        twait(row_name, row_val)
        twait("s_b0", NE)
        mm = g.tensor.matmul(ps[:, 0:K], tile(0), Y0, True, stop and ntiles == 1)
        if ntiles == 2:
            twait("s_y1", NE)
            mm = g.tensor.matmul(ps[:, 0:K], tile(1), Y1, False, stop)
        return mm

    def partial(row_name, row_val, out, ntiles=2):
        group01(T.psc, row_name, row_val, ntiles, True).then_inc(S.mmc, 1)
        vwait(row_name, row_val)
        vwait("mmc", 1)
        g.vector.tensor_tensor(out, T.own[:, 0:K], T.psc[:, 0:K], SUB).then_inc(S.cv, 1)

    def make_eye():
        g.vector.memset(T.ones[:, :], 1.0).then_inc(S.ms, 1)
        g.wait_ge(S.ms, 1)
        g.affine_select(T.eye[:, :], T.ones[:, :], [[-1, P]], AluOpType.is_equal, 0.0, 0, 1).then_inc(S.ey, 1)

    def turn_and_send(tiles, waits, buf, q, dsts):
        pts = {2: T.pt2, 3: T.pt1, 4: T.pt0}
        twait("ey", 1)
        for s, (name, val) in zip(tiles, waits):
            twait(name, val)
            g.tensor.matmul(pts[s][:, 0:P], tile(s), T.eye[:, :], True, True).then_inc(S["tp%d" % s], 1)
        for s in tiles:
            vwait("tp%d" % s, 1)
            g.vector.tensor_copy(T.tt[:, P * (s - 2):P * (s - 1)], pts[s][:, 0:P]).then_inc(S["tc%d" % s], 1)
        for s in tiles:
            g.wait_ge(S["tc%d" % s], 1)
            send(T.tt[:, P * (s - 2):P * (s - 1)], buf[:, P * (s - 2):P * (s - 1)], dsts, S["s_a%d%d" % (q, s)])

    def v_t(s):
        return T.v[:, P * (s - 2):P * (s - 1)]

    def eliminate(r, after_first=None):
        pv = {2: T.pv2, 3: T.pv3, 4: T.pt0}
        at = {5: T.a5t, 4: T.a4t, 3: T.a32t}
        for q in range(r - 1, 2, -1):
            if q == r - 1:
                for name, val in own_sems:
                    twait(name, val)
                rhs = tile(q)
            else:
                twait("vv%d" % q, 1)
                rhs = v_t(q)
            for s in range(q - 1, 1, -1):
                twait("s_a%d%d" % (q, s), NE)
                mm = g.tensor.matmul(pv[s][:, 0:P], at[q][:, P * (s - 2):P * (s - 1)], rhs, q == r - 1, q == s + 1)
                if q == s + 1:
                    mm.then_inc(S["vm%d" % s], 1)
            s = q - 1
            for name, val in own_sems:
                vwait(name, val)
            vwait("vm%d" % s, 1)
            g.vector.tensor_tensor(v_t(s), tile(s), pv[s][:, 0:P], SUB).then_inc(S["vv%d" % s], 1)
            if q == r - 1 and after_first is not None:
                after_first()

    def last_group(terms, opened, c_ap, c_name, c_val):
        for i, (lhs, rhs, waits) in enumerate(terms):
            for name, val in waits:
                twait(name, val)
            mm = g.tensor.matmul(T.pf[:, 0:K], lhs, rhs, i == 0 and not opened, i == len(terms) - 1)
        mm.then_inc(S.mmf, 1)
        vwait(c_name, c_val)
        vwait("mmf", 1)
        g.vector.tensor_tensor(T.yy[:, :], c_ap, T.pf[:, 0:K], SUB).then_inc(S.yv, 1)
        store(T.yy[:, :], S.yv)

    if core == R[0]:
        g.sync.dma_start(T.own[:, 0:K], T.b[:, :]).then_inc(S.ldB, 16)
        g.scalar.dma_start(T.y[:, :], T.b[:, :]).then_inc(S.st, 16)
        g.wait_ge(S.ldB, 16)
        g.remote_dma_fused([transfer(T.own[:, 0:K], Y0, [H1, R[1], H3, R[5], R[6]], S.s_b0),
                            transfer(T.own[:, 0:K], Y0, [H0], S.s_b0, beside=H1)], local_sem=S.sent)
        finish(True)

    elif core == H0:
        g.wait_ge(S.s_b0, NE)
        send(Y0, Y0, [H4a, H4b, R[2]], S.s_b0)
        finish(False)

    elif core in (R[1], H1):
        mine = core == R[1]
        if mine:
            load_b_part(1)
            g.wait_ge(S.ldB, 32)
            send(T.own[:, 0:_col(1)], T.own[:, 0:_col(1)], [H1], S.s_row, ne=NC)
        partial("ldB" if mine else "s_row", 32 if mine else NC, Y1, ntiles=1)
        if mine:
            store(Y1, S.cv)
        g.wait_ge(S.cv, 1)
        send(Y1, Y1, [H3, R[5], R[6]] if mine else [H4a, H4b, R[2]], S.s_y1)
        finish(mine)

    elif core == R[2]:
        load_b_part(2)
        g.wait_ge(S.ldB, 32)
        send(B_PART, B_PART, [H4a], S.s_row)
        partial("ldB", 32, T.yy[:, :])
        store(T.yy[:, :], S.cv)
        finish(True)

    elif core == R[3]:
        make_eye()
        load_a_part(3)
        load_b_part(2)
        g.wait_ge(S.ldB, 32)
        send(B_PART, B_PART, [H3], S.s_row, ne=NC)
        turn_and_send([2], [("ldA", 16)], T.a32t, 3, [H3, R[6], R[5]])
        last_group([(tile(2), C2, [("ldA", 16), ("s_c2", NE)])], False, T.c3[:, :], "s_c3", NE)
        finish(True)

    elif core == H3:
        g.wait_ge(S.s_a32, NE)
        send(T.a32t[:, :], T.a32t[:, :], [R[4]], S.s_a32)
        partial("s_row", NC, T.c3[:, :])
        g.wait_ge(S.cv, 1)
        send(T.c3[:, :], T.c3[:, :], [R[4], R[6], R[5]], S.s_c3)
        send(T.c3[:, :], T.c3[:, :], [R[3]], S.s_c3, beside=R[4])
        finish(False)

    elif core == R[4]:
        load_a_part(4)
        load_b_part(2)
        g.wait_ge(S.ldA, 16)
        g.remote_dma_fused([transfer(tile(3), tile(3), [H4a], S.s_rowA),
                            transfer(tile(2), tile(2), [H4b], S.s_rowA, beside=R[2])], local_sem=S.sent)
        g.wait_ge(S.ldB, 32)
        send(B_PART, B_PART, [H4b], S.s_row, ne=NC)
        eliminate(4)
        last_group([(tile(3), T.c3[:, :], [("s_c3", NE)]),
                    (v_t(2), C2, [("s_c2", NE), ("vv2", 1)])], False, C4, "s_c4", NE)
        finish(True)

    elif core == H4a:
        make_eye()
        turn_and_send([3], [("s_rowA", NE)], T.a4t, 4, [R[6], R[5]])
        partial("s_row", NE, C2)
        g.wait_ge(S.cv, 1)
        send(C2, C2, [R[6], R[5], R[3]], S.s_c2)
        send(C2, C2, [R[4]], S.s_c2, beside=R[6])
        finish(False)

    elif core == H4b:
        make_eye()
        turn_and_send([2], [("s_rowA", NE)], T.a4t, 4, [R[6], R[5]])
        partial("s_row", NC, C4)
        g.wait_ge(S.cv, 1)
        send(C4, C4, [R[6], R[5]], S.s_c4)
        send(C4, C4, [R[4]], S.s_c4, beside=R[6])
        finish(False)

    elif core == R[5]:
        make_eye()
        own_sems[:] = [("ld%d" % s, 16) for s in (4, 3, 2)]
        for s in (4, 3, 2):
            g.sync.dma_start(tile(s), T.l[:, P * s:P * (s + 1)]).then_inc(S["ld%d" % s], 16)
        load_b_part(2)
        turn_and_send([4, 3, 2], own_sems, T.a5t, 5, [R[6]])
        partial("ldB", 32, T.c5[:, :])
        g.wait_ge(S.cv, 1)
        send(T.c5[:, :], T.c5[:, :], [R[6]], S.s_c5)
        eliminate(5)
        last_group([(v_t(3), T.c3[:, :], [("s_c3", NE), ("vv3", 1)]),
                    (v_t(2), C2, [("s_c2", NE), ("vv2", 1)]),
                    (tile(4), C4, [("s_c4", NE)])], False, T.c5[:, :], "cv", 1)
        finish(True)

    elif core == R[6]:
        load_a_part(6)
        load_b_part(2)
        eliminate(6, lambda: group01(T.pf, "ldB", 32, 2, False))
        last_group([(tile(5), T.c5[:, :], [("s_c5", NE)]),
                    (v_t(3), T.c3[:, :], [("s_c3", NE), ("vv3", 1)]),
                    (v_t(2), C2, [("s_c2", NE), ("vv2", 1)]),
                    (v_t(4), C4, [("s_c4", NE), ("vv4", 1)])], True, T.own[:, 0:K], "ldB", 32)
        finish(True)
